import numpy as np, ml_dtypes
CORES = [23,39,55,63,87,103,111,127,18,34,50,58,82,98,106,122]
N = 16
F = 64
def setup_inputs(rng):
    return {"gr": rng.standard_normal((N, 128, N * F), dtype=np.float32).astype(ml_dtypes.bfloat16)}
def setup_inputs_big(rng):
    d = setup_inputs(rng)
    for k in ("gr",): d[k] = (d[k].astype(np.float32) * 1048576.0).astype(d[k].dtype)
    return d
def setup_inputs_small(rng):
    d = setup_inputs(rng)
    for k in ("gr",): d[k] = (d[k].astype(np.float32) * (1 / 1048576.0)).astype(d[k].dtype)
    return d
def setup_inputs_apart(rng):
    d = setup_inputs(rng)
    f = (10.0 ** rng.permutation(np.linspace(-1.5, 1.5, N))).astype(np.float32).reshape(N, 1, 1)
    for k in ("gr",): d[k] = (d[k].astype(np.float32) * f).astype(d[k].dtype)
    return d
def reference(gr):
    s = gr.astype(np.float64).sum(axis=0)
    return {"y": np.stack([s[:, F * r:F * r + F] for r in range(N)]).astype(np.float32 if gr.dtype != np.float64 else np.float64)}

@@ -1,0 +1,140 @@
+from concourse.bass import DstId, RemoteDMATransfer
+from concourse.mybir import AluOpType
+
+N, F, P, SIM = 16, 64, 128, 128
+CAP_ANY = 4
+CAP_SOME = 2
+WMAX = 5
+HOP = 64
+
+SCRATCH = {
+    "G": ("sbuf", [P, N * F], "bfloat16"),
+    "land": ("sbuf", [P, N * F], "bfloat16"),
+    "H": ("sbuf", [P, WMAX * F], "bfloat16"),
+    "res": ("sbuf", [P, F], "float32"),
+    "pa": ("psum", [P, F], "float32"),
+    "pb": ("psum", [P, F], "float32"),
+}
+SEMAPHORES = ["ld", "hin", "sent", "vs", "st"] + ["a%d" % s for s in range(N)]
+
+
+def _bits(mask):
+    return [e for e in range(mask.bit_length()) if (mask >> e) & 1]
+
+
+def _window(cand, cap):
+    best = None
+    for lo in range(N):
+        for w in range(1, min(WMAX, N - lo) + 1):
+            got = [d for d in cand if lo <= d < lo + w][:cap]
+            key = (-len(got), w, lo)
+            if got and (best is None or key < best[0]):
+                best = (key, lo, w, got)
+    return best
+
+
+def _split(items, engines):
+    calls, items = [], list(items)
+    while items:
+        k = 1
+        while k * 2 <= min(len(items), len(engines)):
+            k *= 2
+        per = len(engines) // k
+        calls.append([(d, engines[i * per:(i + 1) * per]) for i, d in enumerate(items[:k])])
+        items = items[k:]
+    return calls
+
+
+def _plan(T, topo):
+    cores = T.cores
+    calls, feed, arrive, clock = {}, {}, dict((d, []) for d in range(N)), {}
+
+    def book(core, call, base):
+        done = []
+        for t in call:
+            end = max(clock.get((core, e), base) for e in t[1]) + P // len(t[1])
+            for e in t[1]:
+                clock[(core, e)] = end
+            done.append(end)
+        calls.setdefault(core, []).append(call)
+        return done
+
+    def blocks(core, s, pairs, buf, lo, base):
+        call = [(cores[d], es, buf, (d - lo) * F, "land", s * F, F, "a%d" % s) for d, es in pairs]
+        for (d, es), end in zip(pairs, book(core, call, base)):
+            arrive[d].append((end, s, len(es)))
+
+    for s, R in enumerate(cores):
+        far = [d for d in range(N) if topo.chip(cores[d]) != topo.chip(R)]
+        home = [d for d in range(N) if d != s and d not in far]
+        helpers = [c for c in range(SIM) if topo.chip(c) == topo.chip(R) and topo.die(c) == topo.die(R)
+                   and T.rank_of(c) is None]
+        helpers.sort(key=lambda h: len([d for d in far if topo.may_write(h, cores[d])]))
+        todo, jobs = list(far), []
+        for h in helpers:
+            can = [d for d in todo if topo.may_write(h, cores[d])]
+            win = _window(can, CAP_ANY if len(can) == len(todo) else CAP_SOME)
+            if win:
+                jobs.append((h, win[1], win[2], win[3]))
+                todo = [d for d in todo if d not in win[3]]
+        jobs.sort(key=lambda j: -len(j[3]))
+        out = _bits(topo.mask(R, cores[far[0]]))
+        stay = [e for e in _bits(topo.mask(R, helpers[0])) if e not in out]
+        todo.sort(key=lambda d: (d - s) % N)
+        direct = _split(todo, out)
+        direct[-1] = direct[-1] + [(d, stay) for d in home]
+        hand = [[(h, stay, "G", lo * F, "H", 0, w * F, "hin")] for h, lo, w, _ in jobs]
+        got = {}
+        for kind, i in [("h", 0), ("d", 0)] + [("h", i) for i in range(1, len(hand))] + \
+                       [("d", i) for i in range(1, len(direct))]:
+            if kind == "h":
+                got[i] = book(R, hand[i], 0)[0]
+            else:
+                blocks(R, s, direct[i], "G", 0, 0)
+        for i, (h, lo, w, picks) in enumerate(jobs):
+            feed[h] = len(stay)
+            for pairs in _split(picks, _bits(topo.mask(h, cores[picks[0]]))):
+                blocks(h, s, pairs, "H", lo, got[i] + HOP)
+    return calls, feed, arrive
+
+
+def _send(g, T, topo, calls):
+    total = 0
+    for call in calls:
+        trs = []
+        for dst, es, sbuf, scol, dbuf, dcol, w, sem in call:
+            rid, pid, _ = topo.addr(dst)
+            trs.append(RemoteDMATransfer(dst_ids=[DstId(rid=rid, pnc=pid)], dma_engine_mask=sum(1 << e for e in es),
+                                         remote_sem=T.sem[sem], src=T[sbuf][:, scol:scol + w],
+                                         dst=T[dbuf][:, dcol:dcol + w]))
+            total += len(es)
+        g.remote_dma_fused(trs, local_sem=T.sem.sent)
+    return total
+
+
+def rank_program(g, core, T, topo):
+    calls, feed, arrive = _plan(T, topo)
+    r = T.rank_of(core)
+    if r is None:
+        if core in feed:
+            g.wait_ge(T.sem.hin, feed[core])
+            g.wait_ge(T.sem.sent, _send(g, T, topo, calls[core]))
+        return
+    g.sync.dma_start(T.G[:], T.gr[:]).then_inc(T.sem.ld, 16)
+    g.wait_ge(T.sem.ld, 16)
+    total = _send(g, T, topo, calls[core])
+    v = g.vector
+    v.wait_ge(T.sem.ld, 16)
+    acc = T.G[:, r * F:(r + 1) * F]
+    order = sorted(arrive[r])
+    for i, (_, s, n) in enumerate(order):
+        v.wait_ge(T.sem["a%d" % s], n)
+        if i:
+            v.wait_ge(T.sem.vs, i)
+        out = T.res[:] if i == len(order) - 1 else (T.pa, T.pb)[i % 2][:]
+        v.tensor_tensor(out, acc, T.land[:, s * F:(s + 1) * F], AluOpType.add).then_inc(T.sem.vs, 1)
+        acc = out
+    g.sync.wait_ge(T.sem.vs, len(order))
+    g.sync.dma_start(T.y[:], T.res[:]).then_inc(T.sem.st, 16)
+    g.sync.wait_ge(T.sem.st, 16)
+    g.wait_ge(T.sem.sent, total)

@@ -1,36 +1,70 @@
 from concourse.bass import DstId, RemoteDMATransfer
-from concourse.mybir import AluOpType
 
 N, F, P, SIM = 16, 64, 128, 128
+HALF = N // 2
 CAP_ANY = 4
 CAP_SOME = 2
 WMAX = 5
 HOP = 64
+ZP = 16
 
 SCRATCH = {
     "G": ("sbuf", [P, N * F], "bfloat16"),
     "land": ("sbuf", [P, N * F], "bfloat16"),
     "H": ("sbuf", [P, WMAX * F], "bfloat16"),
+    "Z": ("sbuf", [ZP, (P + 1) * P // ZP], "bfloat16"),
+    "D": ("dram", [P + 1, P], "bfloat16"),
+    "I": ("sbuf", [P, P], "bfloat16"),
     "res": ("sbuf", [P, F], "float32"),
     "pa": ("psum", [P, F], "float32"),
-    "pb": ("psum", [P, F], "float32"),
 }
-SEMAPHORES = ["ld", "hin", "sent", "vs", "st"] + ["a%d" % s for s in range(N)]
+SEMAPHORES = ["ld0", "ld1", "hin", "sent", "ms", "i1", "i2", "pe", "vs", "st"] + ["a%d" % s for s in range(N)]
+_CACHE = {}
 
 
 def _bits(mask):
     return [e for e in range(mask.bit_length()) if (mask >> e) & 1]
 
 
-def _window(cand, cap):
-    best = None
-    for lo in range(N):
+def _windows(cand, cap):
+    wins = []
+    for lo in cand:
         for w in range(1, min(WMAX, N - lo) + 1):
-            got = [d for d in cand if lo <= d < lo + w][:cap]
-            key = (-len(got), w, lo)
-            if got and (best is None or key < best[0]):
-                best = (key, lo, w, got)
-    return best
+            got = [d for d in cand if lo <= d < lo + w]
+            if len(got) <= cap and got[-1] == lo + w - 1:
+                wins.append((lo, w, got))
+    most = max([len(x[2]) for x in wins] + [0])
+    return [x for x in wins if len(x[2]) == most]
+
+
+def _share(s, far, helpers, can, load):
+    best, lead = None, helpers[-1]
+
+    def combos(todo, hs):
+        if not hs:
+            return [([], todo)]
+        res = []
+        for lo, w, got in _windows([d for d in todo if d in can[hs[0]]], CAP_SOME):
+            for jobs, left in combos([d for d in todo if d not in got], hs[1:]):
+                res.append(([(hs[0], lo, w, got)] + jobs, left))
+        return res or combos(todo, hs[1:])
+
+    alone = [d for d in can[lead] if not [h for h in helpers[:-1] if d in can[h]]]
+    for lo, w, picks in _windows(can[lead], CAP_ANY) + _windows(alone, CAP_ANY):
+        if lo // HALF != (lo + w - 1) // HALF:
+            continue
+        for others, todo in combos([d for d in far if d not in picks], helpers[:-1]):
+            early = len([d for d in todo if d // HALF == lo // HALF])
+            ncalls = sum(bin(n).count("1") for n in (early, len(todo) - early, len(picks)))
+            passed = picks + [d for j in others for d in j[3]]
+            key = (len(todo), 0 if early else 1, 2 * ncalls + 2 * max(j[2] for j in others) + w,
+                   max(load[d] for d in passed), sum(load[d] for d in passed), (lo - s) % N)
+            if best is None or key < best[0]:
+                best = (key, [(lead, lo, w, picks)] + others, todo)
+    for j in best[1]:
+        for d in j[3]:
+            load[d] += 1
+    return best[1], best[2]
 
 
 def _split(items, engines):
@@ -47,7 +81,8 @@ def _split(items, engines):
 
 def _plan(T, topo):
     cores = T.cores
-    calls, feed, arrive, clock = {}, {}, dict((d, []) for d in range(N)), {}
+    calls, feed, arrive, clock, first = {}, {}, dict((d, []) for d in range(N)), {}, {}
+    load, last = [0] * N, [0] * N
 
     def book(core, call, base):
         done = []
@@ -59,50 +94,67 @@ def _plan(T, topo):
         calls.setdefault(core, []).append(call)
         return done
 
+    def hops(a, b):
+        a, b = topo.chip(a), topo.chip(b)
+        return 0 if a == b else 1 if topo.mates(a, b) or topo.same_plane(a, b) else 2
+
     def blocks(core, s, pairs, buf, lo, base):
         call = [(cores[d], es, buf, (d - lo) * F, "land", s * F, F, "a%d" % s) for d, es in pairs]
         for (d, es), end in zip(pairs, book(core, call, base)):
-            arrive[d].append((end, s, len(es)))
+            arrive[d].append((end, hops(core, cores[d]), s, len(es)))
 
     for s, R in enumerate(cores):
         far = [d for d in range(N) if topo.chip(cores[d]) != topo.chip(R)]
         home = [d for d in range(N) if d != s and d not in far]
         helpers = [c for c in range(SIM) if topo.chip(c) == topo.chip(R) and topo.die(c) == topo.die(R)
                    and T.rank_of(c) is None]
-        helpers.sort(key=lambda h: len([d for d in far if topo.may_write(h, cores[d])]))
-        todo, jobs = list(far), []
-        for h in helpers:
-            can = [d for d in todo if topo.may_write(h, cores[d])]
-            win = _window(can, CAP_ANY if len(can) == len(todo) else CAP_SOME)
-            if win:
-                jobs.append((h, win[1], win[2], win[3]))
-                todo = [d for d in todo if d not in win[3]]
-        jobs.sort(key=lambda j: -len(j[3]))
+        can = dict((h, [d for d in far if topo.may_write(h, cores[d])]) for h in helpers)
+        helpers.sort(key=lambda h: len(can[h]))
+        jobs, todo = _share(s, far, helpers, can, load)
+        first[s] = jobs[0][1] // HALF
+        wide = max(j[2] for j in jobs[1:])
+        jobs = jobs[:1] + [(h, min(lo, N - wide), wide, picks) for h, lo, _, picks in jobs[1:]]
         out = _bits(topo.mask(R, cores[far[0]]))
         stay = [e for e in _bits(topo.mask(R, helpers[0])) if e not in out]
         todo.sort(key=lambda d: (d - s) % N)
-        direct = _split(todo, out)
-        direct[-1] = direct[-1] + [(d, stay) for d in home]
-        hand = [[(h, stay, "G", lo * F, "H", 0, w * F, "hin")] for h, lo, w, _ in jobs]
+        early = _split([d for d in todo if d // HALF == first[s]], out)
+        late = _split([d for d in todo if d // HALF != first[s]], out)
+        late[-1] = late[-1] + [(d, stay) for d in home]
         got = {}
-        for kind, i in [("h", 0), ("d", 0)] + [("h", i) for i in range(1, len(hand))] + \
-                       [("d", i) for i in range(1, len(direct))]:
-            if kind == "h":
-                got[i] = book(R, hand[i], 0)[0]
-            else:
-                blocks(R, s, direct[i], "G", 0, 0)
-        for i, (h, lo, w, picks) in enumerate(jobs):
-            feed[h] = len(stay)
-            for pairs in _split(picks, _bits(topo.mask(h, cores[picks[0]]))):
-                blocks(h, s, pairs, "H", lo, got[i] + HOP)
-    return calls, feed, arrive
+
+        def hand(pairs):
+            call = [(j[0], es, "G", j[1] * F, "H", 0, j[2] * F, "hin") for j, es in pairs]
+            for (j, es), end in zip(pairs, book(R, call, 0)):
+                got[j[0]], feed[j[0]] = end, len(es)
+
+        hand([(jobs[0], stay)])
+        for pairs in early + late[:1]:
+            blocks(R, s, pairs, "G", 0, 0)
+        for pairs in _split(jobs[1:], stay):
+            hand(pairs)
+        for pairs in late[1:]:
+            blocks(R, s, pairs, "G", 0, 0)
+        for h, lo, w, picks in jobs:
+            picks = sorted(picks, key=lambda d: -last[d])
+            cut = (len(picks) + 1) // 2
+            for d in picks[cut:] or picks:
+                last[d] += 1
+            for part in (picks[:cut], picks[cut:]):
+                for pairs in _split(part, _bits(topo.mask(h, cores[picks[0]]))):
+                    blocks(h, s, pairs, "H", lo, got[h] + HOP)
+    return calls, feed, arrive, first
 
 
 def _send(g, T, topo, calls):
-    total = 0
+    total, have = 0, []
     for call in calls:
         trs = []
         for dst, es, sbuf, scol, dbuf, dcol, w, sem in call:
+            if sbuf == "G":
+                for h in range(scol // (HALF * F), (scol + w - 1) // (HALF * F) + 1):
+                    if h not in have:
+                        g.wait_ge(T.sem["ld%d" % h], 16)
+                        have.append(h)
             rid, pid, _ = topo.addr(dst)
             trs.append(RemoteDMATransfer(dst_ids=[DstId(rid=rid, pnc=pid)], dma_engine_mask=sum(1 << e for e in es),
                                          remote_sem=T.sem[sem], src=T[sbuf][:, scol:scol + w],
@@ -113,28 +165,38 @@ def _send(g, T, topo, calls):
 
 
 def rank_program(g, core, T, topo):
-    calls, feed, arrive = _plan(T, topo)
+    if "plan" not in _CACHE:
+        _CACHE["plan"] = _plan(T, topo)
+    calls, feed, arrive, first = _CACHE["plan"]
     r = T.rank_of(core)
     if r is None:
         if core in feed:
             g.wait_ge(T.sem.hin, feed[core])
             g.wait_ge(T.sem.sent, _send(g, T, topo, calls[core]))
         return
-    g.sync.dma_start(T.G[:], T.gr[:]).then_inc(T.sem.ld, 16)
-    g.wait_ge(T.sem.ld, 16)
+    for q, h in ((g.sync, first[r]), (g.scalar, 1 - first[r])):
+        cols = slice(h * HALF * F, (h + 1) * HALF * F)
+        q.dma_start(T.G[:, cols], T.gr[:, cols]).then_inc(T.sem["ld%d" % h], 16)
+    v, pe = g.vector, g.tensor
+    v.memset(T.Z[:], 0.0).then_inc(T.sem.ms, 1)
+    v.wait_ge(T.sem.ms, 1)
+    v.memset(T.Z[:, 0:(P + 1) * P // ZP:P + 1], 1.0).then_inc(T.sem.ms, 1)
+    g.scalar.wait_ge(T.sem.ms, 2)
+    g.scalar.dma_start(T.D[:], T.Z[:]).then_inc(T.sem.i1, 16)
+    g.scalar.wait_ge(T.sem.i1, 16)
+    g.scalar.dma_start(T.I[:], T.D[0:P, :]).then_inc(T.sem.i2, 16)
     total = _send(g, T, topo, calls[core])
-    v = g.vector
-    v.wait_ge(T.sem.ld, 16)
-    acc = T.G[:, r * F:(r + 1) * F]
     order = sorted(arrive[r])
-    for i, (_, s, n) in enumerate(order):
-        v.wait_ge(T.sem["a%d" % s], n)
-        if i:
-            v.wait_ge(T.sem.vs, i)
-        out = T.res[:] if i == len(order) - 1 else (T.pa, T.pb)[i % 2][:]
-        v.tensor_tensor(out, acc, T.land[:, s * F:(s + 1) * F], AluOpType.add).then_inc(T.sem.vs, 1)
-        acc = out
-    g.sync.wait_ge(T.sem.vs, len(order))
+    pe.wait_ge(T.sem.i2, 16)
+    pe.wait_ge(T.sem["ld%d" % (r // HALF)], 16)
+    pe.matmul(T.pa[:], T.I[:], T.G[:, r * F:(r + 1) * F], True, False)
+    for i, (_, _, s, n) in enumerate(order):
+        pe.wait_ge(T.sem["a%d" % s], n)
+        mm = pe.matmul(T.pa[:], T.I[:], T.land[:, s * F:(s + 1) * F], False, i == len(order) - 1)
+    mm.then_inc(T.sem.pe, 1)
+    v.wait_ge(T.sem.pe, 1)
+    v.tensor_copy(T.res[:], T.pa[:]).then_inc(T.sem.vs, 1)
+    g.sync.wait_ge(T.sem.vs, 1)
     g.sync.dma_start(T.y[:], T.res[:]).then_inc(T.sem.st, 16)
     g.sync.wait_ge(T.sem.st, 16)
     g.wait_ge(T.sem.sent, total)

@@ -2,16 +2,16 @@ from concourse.bass import DstId, RemoteDMATransfer
 
 N, F, P, SIM = 16, 64, 128, 128
 HALF = N // 2
-CAP_ANY = 4
-CAP_SOME = 2
+CAPS = (1, 2, 5)
 WMAX = 5
+WLEAD = 6
 HOP = 64
-ZP = 16
+ZP = 32
 
 SCRATCH = {
     "G": ("sbuf", [P, N * F], "bfloat16"),
     "land": ("sbuf", [P, N * F], "bfloat16"),
-    "H": ("sbuf", [P, WMAX * F], "bfloat16"),
+    "H": ("sbuf", [P, WLEAD * F], "bfloat16"),
     "Z": ("sbuf", [ZP, (P + 1) * P // ZP], "bfloat16"),
     "D": ("dram", [P + 1, P], "bfloat16"),
     "I": ("sbuf", [P, P], "bfloat16"),
@@ -26,10 +26,10 @@ def _bits(mask):
     return [e for e in range(mask.bit_length()) if (mask >> e) & 1]
 
 
-def _windows(cand, cap):
+def _windows(cand, cap, wmax=WMAX):
     wins = []
     for lo in cand:
-        for w in range(1, min(WMAX, N - lo) + 1):
+        for w in range(1, min(wmax, N - lo) + 1):
             got = [d for d in cand if lo <= d < lo + w]
             if len(got) <= cap and got[-1] == lo + w - 1:
                 wins.append((lo, w, got))
@@ -44,23 +44,23 @@ def _share(s, far, helpers, can, load):
         if not hs:
             return [([], todo)]
         res = []
-        for lo, w, got in _windows([d for d in todo if d in can[hs[0]]], CAP_SOME):
+        for lo, w, got in _windows([d for d in todo if d in can[hs[0]]], CAPS[helpers.index(hs[0])]):
             for jobs, left in combos([d for d in todo if d not in got], hs[1:]):
                 res.append(([(hs[0], lo, w, got)] + jobs, left))
         return res or combos(todo, hs[1:])
 
     alone = [d for d in can[lead] if not [h for h in helpers[:-1] if d in can[h]]]
-    for lo, w, picks in _windows(can[lead], CAP_ANY) + _windows(alone, CAP_ANY):
+    for lo, w, picks in _windows(can[lead], CAPS[-1], WLEAD) + _windows(alone, CAPS[-1], WLEAD):
         if lo // HALF != (lo + w - 1) // HALF:
             continue
         for others, todo in combos([d for d in far if d not in picks], helpers[:-1]):
             early = len([d for d in todo if d // HALF == lo // HALF])
-            ncalls = sum(bin(n).count("1") for n in (early, len(todo) - early, len(picks)))
+            ncalls = sum(bin(n).count("1") for n in (early, len(todo) - early))
             passed = picks + [d for j in others for d in j[3]]
-            key = (len(todo), 0 if early else 1, 2 * ncalls + 2 * max(j[2] for j in others) + w,
+            key = (len(todo), 0 if early else 1, 2 * ncalls + sum(j[2] for j in others) + w,
                    max(load[d] for d in passed), sum(load[d] for d in passed), (lo - s) % N)
             if best is None or key < best[0]:
-                best = (key, [(lead, lo, w, picks)] + others, todo)
+                best = (key, [(lead, lo, w, picks)] + sorted(others, key=lambda j: -len(j[3])), todo)
     for j in best[1]:
         for d in j[3]:
             load[d] += 1
@@ -81,7 +81,7 @@ def _split(items, engines):
 
 def _plan(T, topo):
     cores = T.cores
-    calls, feed, arrive, clock, first = {}, {}, dict((d, []) for d in range(N)), {}, {}
+    calls, feed, arrive, clock, first, maker = {}, {}, dict((d, []) for d in range(N)), {}, {}, {}
     load, last = [0] * N, [0] * N
 
     def book(core, call, base):
@@ -112,37 +112,35 @@ def _plan(T, topo):
         helpers.sort(key=lambda h: len(can[h]))
         jobs, todo = _share(s, far, helpers, can, load)
         first[s] = jobs[0][1] // HALF
-        wide = max(j[2] for j in jobs[1:])
-        jobs = jobs[:1] + [(h, min(lo, N - wide), wide, picks) for h, lo, _, picks in jobs[1:]]
+        maker[jobs[0][0]] = (R, _bits(topo.mask(jobs[0][0], cores[far[0]])))
         out = _bits(topo.mask(R, cores[far[0]]))
         stay = [e for e in _bits(topo.mask(R, helpers[0])) if e not in out]
-        todo.sort(key=lambda d: (d - s) % N)
+        todo.sort(key=lambda d: (-hops(R, cores[d]), (d - s) % N))
         early = _split([d for d in todo if d // HALF == first[s]], out)
         late = _split([d for d in todo if d // HALF != first[s]], out)
         late[-1] = late[-1] + [(d, stay) for d in home]
         got = {}
 
-        def hand(pairs):
-            call = [(j[0], es, "G", j[1] * F, "H", 0, j[2] * F, "hin") for j, es in pairs]
-            for (j, es), end in zip(pairs, book(R, call, 0)):
-                got[j[0]], feed[j[0]] = end, len(es)
+        def hand(j):
+            got[j[0]] = book(R, [(j[0], stay, "G", j[1] * F, "H", 0, j[2] * F, "hin")], 0)[0]
+            feed[j[0]] = len(stay)
 
-        hand([(jobs[0], stay)])
-        for pairs in early + late[:1]:
+        hand(jobs[0])
+        for pairs in early:
             blocks(R, s, pairs, "G", 0, 0)
-        for pairs in _split(jobs[1:], stay):
-            hand(pairs)
-        for pairs in late[1:]:
+        for j in jobs[1:]:
+            hand(j)
+        for pairs in late:
             blocks(R, s, pairs, "G", 0, 0)
         for h, lo, w, picks in jobs:
-            picks = sorted(picks, key=lambda d: -last[d])
+            picks = sorted(picks, key=lambda d: (-hops(h, cores[d]), -last[d]))
             cut = (len(picks) + 1) // 2
             for d in picks[cut:] or picks:
                 last[d] += 1
             for part in (picks[:cut], picks[cut:]):
                 for pairs in _split(part, _bits(topo.mask(h, cores[picks[0]]))):
                     blocks(h, s, pairs, "H", lo, got[h] + HOP)
-    return calls, feed, arrive, first
+    return calls, feed, arrive, first, maker
 
 
 def _send(g, T, topo, calls):
@@ -167,27 +165,35 @@ def _send(g, T, topo, calls):
 def rank_program(g, core, T, topo):
     if "plan" not in _CACHE:
         _CACHE["plan"] = _plan(T, topo)
-    calls, feed, arrive, first = _CACHE["plan"]
+    calls, feed, arrive, first, maker = _CACHE["plan"]
     r = T.rank_of(core)
+    v, pe = g.vector, g.tensor
     if r is None:
-        if core in feed:
-            g.wait_ge(T.sem.hin, feed[core])
-            g.wait_ge(T.sem.sent, _send(g, T, topo, calls[core]))
+        if core not in feed:
+            return
+        total = 0
+        if core in maker:
+            R, es = maker[core]
+            v.memset(T.Z[:], 0.0).then_inc(T.sem.ms, 1)
+            v.wait_ge(T.sem.ms, 1)
+            v.memset(T.Z[:, 0:(P + 1) * P // ZP:P + 1], 1.0).then_inc(T.sem.ms, 1)
+            g.sync.wait_ge(T.sem.ms, 2)
+            g.sync.dma_start(T.D[:], T.Z[:]).then_inc(T.sem.i1, 16)
+            g.wait_ge(T.sem.i1, 16)
+            rid, pid, _ = topo.addr(R)
+            g.remote_dma_fused([RemoteDMATransfer(dst_ids=[DstId(rid=rid, pnc=pid)],
+                                                  dma_engine_mask=sum(1 << e for e in es), remote_sem=T.sem.i2,
+                                                  src=T.D[0:P, :], dst=T.I[:])], local_sem=T.sem.sent)
+            total = len(es)
+        g.wait_ge(T.sem.hin, feed[core])
+        g.wait_ge(T.sem.sent, total + _send(g, T, topo, calls[core]))
         return
     for q, h in ((g.sync, first[r]), (g.scalar, 1 - first[r])):
         cols = slice(h * HALF * F, (h + 1) * HALF * F)
         q.dma_start(T.G[:, cols], T.gr[:, cols]).then_inc(T.sem["ld%d" % h], 16)
-    v, pe = g.vector, g.tensor
-    v.memset(T.Z[:], 0.0).then_inc(T.sem.ms, 1)
-    v.wait_ge(T.sem.ms, 1)
-    v.memset(T.Z[:, 0:(P + 1) * P // ZP:P + 1], 1.0).then_inc(T.sem.ms, 1)
-    g.scalar.wait_ge(T.sem.ms, 2)
-    g.scalar.dma_start(T.D[:], T.Z[:]).then_inc(T.sem.i1, 16)
-    g.scalar.wait_ge(T.sem.i1, 16)
-    g.scalar.dma_start(T.I[:], T.D[0:P, :]).then_inc(T.sem.i2, 16)
     total = _send(g, T, topo, calls[core])
     order = sorted(arrive[r])
-    pe.wait_ge(T.sem.i2, 16)
+    pe.wait_ge(T.sem.i2, [len(es) for R, es in maker.values() if R == core][0])
     pe.wait_ge(T.sem["ld%d" % (r // HALF)], 16)
     pe.matmul(T.pa[:], T.I[:], T.G[:, r * F:(r + 1) * F], True, False)
     for i, (_, _, s, n) in enumerate(order):

@@ -1,24 +1,24 @@
 from concourse.bass import DstId, RemoteDMATransfer
+from concourse.mybir import AluOpType
 
 N, F, P, SIM = 16, 64, 128, 128
 HALF = N // 2
-CAPS = (1, 2, 5)
+CAPS = (2, 3, 4)
+IW = 32
 WMAX = 5
 WLEAD = 6
 HOP = 64
-ZP = 32
 
 SCRATCH = {
     "G": ("sbuf", [P, N * F], "bfloat16"),
     "land": ("sbuf", [P, N * F], "bfloat16"),
     "H": ("sbuf", [P, WLEAD * F], "bfloat16"),
-    "Z": ("sbuf", [ZP, (P + 1) * P // ZP], "bfloat16"),
-    "D": ("dram", [P + 1, P], "bfloat16"),
+    "Ip": ("sbuf", [P, IW], "bfloat16"),
     "I": ("sbuf", [P, P], "bfloat16"),
     "res": ("sbuf", [P, F], "float32"),
     "pa": ("psum", [P, F], "float32"),
 }
-SEMAPHORES = ["ld0", "ld1", "hin", "sent", "ms", "i1", "i2", "pe", "vs", "st"] + ["a%d" % s for s in range(N)]
+SEMAPHORES = ["ld0", "ld1", "hin", "sent", "ms", "af", "i2", "pe", "vs", "st"] + ["a%d" % s for s in range(N)]
 _CACHE = {}
 
 
@@ -37,20 +37,20 @@ def _windows(cand, cap, wmax=WMAX):
     return [x for x in wins if len(x[2]) == most]
 
 
-def _share(s, far, helpers, can, load):
+def _share(s, far, helpers, can, load, caps):
     best, lead = None, helpers[-1]
 
     def combos(todo, hs):
         if not hs:
             return [([], todo)]
         res = []
-        for lo, w, got in _windows([d for d in todo if d in can[hs[0]]], CAPS[helpers.index(hs[0])]):
+        for lo, w, got in _windows([d for d in todo if d in can[hs[0]]], caps[helpers.index(hs[0])]):
             for jobs, left in combos([d for d in todo if d not in got], hs[1:]):
                 res.append(([(hs[0], lo, w, got)] + jobs, left))
         return res or combos(todo, hs[1:])
 
     alone = [d for d in can[lead] if not [h for h in helpers[:-1] if d in can[h]]]
-    for lo, w, picks in _windows(can[lead], CAPS[-1], WLEAD) + _windows(alone, CAPS[-1], WLEAD):
+    for lo, w, picks in _windows(can[lead], caps[-1], WLEAD) + _windows(alone, caps[-1], WLEAD):
         if lo // HALF != (lo + w - 1) // HALF:
             continue
         for others, todo in combos([d for d in far if d not in picks], helpers[:-1]):
@@ -110,26 +110,31 @@ def _plan(T, topo):
                    and T.rank_of(c) is None]
         can = dict((h, [d for d in far if topo.may_write(h, cores[d])]) for h in helpers)
         helpers.sort(key=lambda h: len(can[h]))
-        jobs, todo = _share(s, far, helpers, can, load)
+        caps = tuple(min(c, len(can[h]) // (len(helpers) - 1)) for c, h in zip(CAPS, helpers[:-1])) + CAPS[-1:]
+        jobs, todo = _share(s, far, helpers, can, load, caps)
         first[s] = jobs[0][1] // HALF
-        maker[jobs[0][0]] = (R, _bits(topo.mask(jobs[0][0], cores[far[0]])))
         out = _bits(topo.mask(R, cores[far[0]]))
         stay = [e for e in _bits(topo.mask(R, helpers[0])) if e not in out]
+        for i, j in enumerate(jobs):
+            maker[j[0]] = (R, i * IW, [_bits(topo.mask(j[0], cores[far[0]]))])
+        maker[cores[home[0]]] = (R, len(jobs) * IW, [stay, out])
         todo.sort(key=lambda d: (-hops(R, cores[d]), (d - s) % N))
         early = _split([d for d in todo if d // HALF == first[s]], out)
-        late = _split([d for d in todo if d // HALF != first[s]], out)
+        late = _split([d for d in todo if d // HALF != first[s]], out) or [[]]
         late[-1] = late[-1] + [(d, stay) for d in home]
         got = {}
 
-        def hand(j):
-            got[j[0]] = book(R, [(j[0], stay, "G", j[1] * F, "H", 0, j[2] * F, "hin")], 0)[0]
-            feed[j[0]] = len(stay)
+        def hand(j, es):
+            got[j[0]] = book(R, [(j[0], es, "G", j[1] * F, "H", 0, j[2] * F, "hin")], 0)[0]
+            feed[j[0]] = len(es)
 
-        hand(jobs[0])
+        soon = [j for j in jobs if j[1] // HALF == first[s] == (j[1] + j[2] - 1) // HALF]
+        for j in soon:
+            hand(j, stay)
         for pairs in early:
             blocks(R, s, pairs, "G", 0, 0)
-        for j in jobs[1:]:
-            hand(j)
+        for j in [j for j in jobs if j not in soon]:
+            hand(j, stay)
         for pairs in late:
             blocks(R, s, pairs, "G", 0, 0)
         for h, lo, w, picks in jobs:
@@ -168,32 +173,32 @@ def rank_program(g, core, T, topo):
     calls, feed, arrive, first, maker = _CACHE["plan"]
     r = T.rank_of(core)
     v, pe = g.vector, g.tensor
+    if r is None and core not in feed:
+        return
+    if r is not None:
+        for q, h in ((g.sync, first[r]), (g.scalar, 1 - first[r])):
+            cols = slice(h * HALF * F, (h + 1) * HALF * F)
+            q.dma_start(T.G[:, cols], T.gr[:, cols]).then_inc(T.sem["ld%d" % h], 16)
+    R, c0, groups = maker[core]
+    v.memset(T.Ip[:], 1.0).then_inc(T.sem.ms, 1)
+    g.wait_ge(T.sem.ms, 1)
+    g.affine_select(T.Ip[:], T.Ip[:], [[-1, IW]], AluOpType.is_equal, 0.0, -c0, 1).then_inc(T.sem.af, 1)
+    g.wait_ge(T.sem.af, 1)
+    rid, pid, _ = topo.addr(R)
+    total, w = 0, IW // len(groups)
+    for i, es in enumerate(groups):
+        g.remote_dma_fused([RemoteDMATransfer(dst_ids=[DstId(rid=rid, pnc=pid)],
+                                              dma_engine_mask=sum(1 << e for e in es), remote_sem=T.sem.i2,
+                                              src=T.Ip[:, i * w:(i + 1) * w],
+                                              dst=T.I[:, c0 + i * w:c0 + (i + 1) * w])], local_sem=T.sem.sent)
+        total += len(es)
     if r is None:
-        if core not in feed:
-            return
-        total = 0
-        if core in maker:
-            R, es = maker[core]
-            v.memset(T.Z[:], 0.0).then_inc(T.sem.ms, 1)
-            v.wait_ge(T.sem.ms, 1)
-            v.memset(T.Z[:, 0:(P + 1) * P // ZP:P + 1], 1.0).then_inc(T.sem.ms, 1)
-            g.sync.wait_ge(T.sem.ms, 2)
-            g.sync.dma_start(T.D[:], T.Z[:]).then_inc(T.sem.i1, 16)
-            g.wait_ge(T.sem.i1, 16)
-            rid, pid, _ = topo.addr(R)
-            g.remote_dma_fused([RemoteDMATransfer(dst_ids=[DstId(rid=rid, pnc=pid)],
-                                                  dma_engine_mask=sum(1 << e for e in es), remote_sem=T.sem.i2,
-                                                  src=T.D[0:P, :], dst=T.I[:])], local_sem=T.sem.sent)
-            total = len(es)
         g.wait_ge(T.sem.hin, feed[core])
         g.wait_ge(T.sem.sent, total + _send(g, T, topo, calls[core]))
         return
-    for q, h in ((g.sync, first[r]), (g.scalar, 1 - first[r])):
-        cols = slice(h * HALF * F, (h + 1) * HALF * F)
-        q.dma_start(T.G[:, cols], T.gr[:, cols]).then_inc(T.sem["ld%d" % h], 16)
-    total = _send(g, T, topo, calls[core])
+    total += _send(g, T, topo, calls[core])
     order = sorted(arrive[r])
-    pe.wait_ge(T.sem.i2, [len(es) for R, es in maker.values() if R == core][0])
+    pe.wait_ge(T.sem.i2, sum(len(es) for R, _, groups in maker.values() if R == core for es in groups))
     pe.wait_ge(T.sem["ld%d" % (r // HALF)], 16)
     pe.matmul(T.pa[:], T.I[:], T.G[:, r * F:(r + 1) * F], True, False)
     for i, (_, _, s, n) in enumerate(order):

from concourse.bass import DstId, RemoteDMATransfer
from concourse.mybir import AluOpType

N, F, P, SIM = 16, 64, 128, 128
HALF = N // 2
CAPS = (2, 3, 4)
IW = 32
WMAX = 5
WLEAD = 6
HOP = 64

SCRATCH = {
    "G": ("sbuf", [P, N * F], "bfloat16"),
    "land": ("sbuf", [P, N * F], "bfloat16"),
    "H": ("sbuf", [P, WLEAD * F], "bfloat16"),
    "Ip": ("sbuf", [P, IW], "bfloat16"),
    "I": ("sbuf", [P, P], "bfloat16"),
    "res": ("sbuf", [P, F], "float32"),
    "pa": ("psum", [P, F], "float32"),
}
SEMAPHORES = ["ld0", "ld1", "hin", "sent", "ms", "af", "i2", "pe", "vs", "st"] + ["a%d" % s for s in range(N)]
_CACHE = {}


def _bits(mask):
    return [e for e in range(mask.bit_length()) if (mask >> e) & 1]


def _windows(cand, cap, wmax=WMAX):
    wins = []
    for lo in cand:
        for w in range(1, min(wmax, N - lo) + 1):
            got = [d for d in cand if lo <= d < lo + w]
            if len(got) <= cap and got[-1] == lo + w - 1:
                wins.append((lo, w, got))
    most = max([len(x[2]) for x in wins] + [0])
    return [x for x in wins if len(x[2]) == most]


def _share(s, far, helpers, can, load, caps):
    best, lead = None, helpers[-1]

    def combos(todo, hs):
        if not hs:
            return [([], todo)]
        res = []
        for lo, w, got in _windows([d for d in todo if d in can[hs[0]]], caps[helpers.index(hs[0])]):
            for jobs, left in combos([d for d in todo if d not in got], hs[1:]):
                res.append(([(hs[0], lo, w, got)] + jobs, left))
        return res or combos(todo, hs[1:])

    alone = [d for d in can[lead] if not [h for h in helpers[:-1] if d in can[h]]]
    for lo, w, picks in _windows(can[lead], caps[-1], WLEAD) + _windows(alone, caps[-1], WLEAD):
        if lo // HALF != (lo + w - 1) // HALF:
            continue
        for others, todo in combos([d for d in far if d not in picks], helpers[:-1]):
            early = len([d for d in todo if d // HALF == lo // HALF])
            ncalls = sum(bin(n).count("1") for n in (early, len(todo) - early))
            passed = picks + [d for j in others for d in j[3]]
            key = (len(todo), 0 if early else 1, 2 * ncalls + sum(j[2] for j in others) + w,
                   max(load[d] for d in passed), sum(load[d] for d in passed), (lo - s) % N)
            if best is None or key < best[0]:
                best = (key, [(lead, lo, w, picks)] + sorted(others, key=lambda j: -len(j[3])), todo)
    for j in best[1]:
        for d in j[3]:
            load[d] += 1
    return best[1], best[2]


def _split(items, engines):
    calls, items = [], list(items)
    while items:
        k = 1
        while k * 2 <= min(len(items), len(engines)):
            k *= 2
        per = len(engines) // k
        calls.append([(d, engines[i * per:(i + 1) * per]) for i, d in enumerate(items[:k])])
        items = items[k:]
    return calls


def _plan(T, topo):
    cores = T.cores
    calls, feed, arrive, clock, first, maker = {}, {}, dict((d, []) for d in range(N)), {}, {}, {}
    load, last = [0] * N, [0] * N

    def book(core, call, base):
        done = []
        for t in call:
            end = max(clock.get((core, e), base) for e in t[1]) + P // len(t[1])
            for e in t[1]:
                clock[(core, e)] = end
            done.append(end)
        calls.setdefault(core, []).append(call)
        return done

    def hops(a, b):
        a, b = topo.chip(a), topo.chip(b)
        return 0 if a == b else 1 if topo.mates(a, b) or topo.same_plane(a, b) else 2

    def blocks(core, s, pairs, buf, lo, base):
        call = [(cores[d], es, buf, (d - lo) * F, "land", s * F, F, "a%d" % s) for d, es in pairs]
        for (d, es), end in zip(pairs, book(core, call, base)):
            arrive[d].append((end, hops(core, cores[d]), s, len(es)))

    for s, R in enumerate(cores):
        far = [d for d in range(N) if topo.chip(cores[d]) != topo.chip(R)]
        home = [d for d in range(N) if d != s and d not in far]
        helpers = [c for c in range(SIM) if topo.chip(c) == topo.chip(R) and topo.die(c) == topo.die(R)
                   and T.rank_of(c) is None]
        can = dict((h, [d for d in far if topo.may_write(h, cores[d])]) for h in helpers)
        helpers.sort(key=lambda h: len(can[h]))
        caps = tuple(min(c, len(can[h]) // (len(helpers) - 1)) for c, h in zip(CAPS, helpers[:-1])) + CAPS[-1:]
        jobs, todo = _share(s, far, helpers, can, load, caps)
        first[s] = jobs[0][1] // HALF
        out = _bits(topo.mask(R, cores[far[0]]))
        stay = [e for e in _bits(topo.mask(R, helpers[0])) if e not in out]
        for i, j in enumerate(jobs):
            maker[j[0]] = (R, i * IW, [_bits(topo.mask(j[0], cores[far[0]]))])
        maker[cores[home[0]]] = (R, len(jobs) * IW, [stay, out])
        todo.sort(key=lambda d: (-hops(R, cores[d]), (d - s) % N))
        early = _split([d for d in todo if d // HALF == first[s]], out)
        late = _split([d for d in todo if d // HALF != first[s]], out) or [[]]
        late[-1] = late[-1] + [(d, stay) for d in home]
        got = {}

        def hand(j, es):
            got[j[0]] = book(R, [(j[0], es, "G", j[1] * F, "H", 0, j[2] * F, "hin")], 0)[0]
            feed[j[0]] = len(es)

        soon = [j for j in jobs if j[1] // HALF == first[s] == (j[1] + j[2] - 1) // HALF]
        for j in soon:
            hand(j, stay)
        for pairs in early:
            blocks(R, s, pairs, "G", 0, 0)
        for j in [j for j in jobs if j not in soon]:
            hand(j, stay)
        for pairs in late:
            blocks(R, s, pairs, "G", 0, 0)
        for h, lo, w, picks in jobs:
            picks = sorted(picks, key=lambda d: (-hops(h, cores[d]), -last[d]))
            cut = (len(picks) + 1) // 2
            for d in picks[cut:] or picks:
                last[d] += 1
            for part in (picks[:cut], picks[cut:]):
                for pairs in _split(part, _bits(topo.mask(h, cores[picks[0]]))):
                    blocks(h, s, pairs, "H", lo, got[h] + HOP)
    return calls, feed, arrive, first, maker


def _send(g, T, topo, calls):
    total, have = 0, []
    for call in calls:
        trs = []
        for dst, es, sbuf, scol, dbuf, dcol, w, sem in call:
            if sbuf == "G":
                for h in range(scol // (HALF * F), (scol + w - 1) // (HALF * F) + 1):
                    if h not in have:
                        g.wait_ge(T.sem["ld%d" % h], 16)
                        have.append(h)
            rid, pid, _ = topo.addr(dst)
            trs.append(RemoteDMATransfer(dst_ids=[DstId(rid=rid, pnc=pid)], dma_engine_mask=sum(1 << e for e in es),
                                         remote_sem=T.sem[sem], src=T[sbuf][:, scol:scol + w],
                                         dst=T[dbuf][:, dcol:dcol + w]))
            total += len(es)
        g.remote_dma_fused(trs, local_sem=T.sem.sent)
    return total


def rank_program(g, core, T, topo):
    if "plan" not in _CACHE:
        _CACHE["plan"] = _plan(T, topo)
    calls, feed, arrive, first, maker = _CACHE["plan"]
    r = T.rank_of(core)
    v, pe = g.vector, g.tensor
    if r is None and core not in feed:
        return
    if r is not None:
        for q, h in ((g.sync, first[r]), (g.scalar, 1 - first[r])):
            cols = slice(h * HALF * F, (h + 1) * HALF * F)
            q.dma_start(T.G[:, cols], T.gr[:, cols]).then_inc(T.sem["ld%d" % h], 16)
    R, c0, groups = maker[core]
    v.memset(T.Ip[:], 1.0).then_inc(T.sem.ms, 1)
    g.wait_ge(T.sem.ms, 1)
    g.affine_select(T.Ip[:], T.Ip[:], [[-1, IW]], AluOpType.is_equal, 0.0, -c0, 1).then_inc(T.sem.af, 1)
    g.wait_ge(T.sem.af, 1)
    rid, pid, _ = topo.addr(R)
    total, w = 0, IW // len(groups)
    for i, es in enumerate(groups):
        g.remote_dma_fused([RemoteDMATransfer(dst_ids=[DstId(rid=rid, pnc=pid)],
                                              dma_engine_mask=sum(1 << e for e in es), remote_sem=T.sem.i2,
                                              src=T.Ip[:, i * w:(i + 1) * w],
                                              dst=T.I[:, c0 + i * w:c0 + (i + 1) * w])], local_sem=T.sem.sent)
        total += len(es)
    if r is None:
        g.wait_ge(T.sem.hin, feed[core])
        g.wait_ge(T.sem.sent, total + _send(g, T, topo, calls[core]))
        return
    total += _send(g, T, topo, calls[core])
    order = sorted(arrive[r])
    pe.wait_ge(T.sem.i2, sum(len(es) for R, _, groups in maker.values() if R == core for es in groups))
    pe.wait_ge(T.sem["ld%d" % (r // HALF)], 16)
    pe.matmul(T.pa[:], T.I[:], T.G[:, r * F:(r + 1) * F], True, False)
    for i, (_, _, s, n) in enumerate(order):
        pe.wait_ge(T.sem["a%d" % s], n)
        mm = pe.matmul(T.pa[:], T.I[:], T.land[:, s * F:(s + 1) * F], False, i == len(order) - 1)
    mm.then_inc(T.sem.pe, 1)
    v.wait_ge(T.sem.pe, 1)
    v.tensor_copy(T.res[:], T.pa[:]).then_inc(T.sem.vs, 1)
    g.sync.wait_ge(T.sem.vs, 1)
    g.sync.dma_start(T.y[:], T.res[:]).then_inc(T.sem.st, 16)
    g.sync.wait_ge(T.sem.st, 16)
    g.wait_ge(T.sem.sent, total)
